import numpy as np
import ml_dtypes


def mxq(x, axis, fmt="e4m3"):
    dtype, down = {"e4m3": (ml_dtypes.float8_e4m3fn, 7), "e5m2": (ml_dtypes.float8_e5m2, 14)}[fmt]
    v = np.moveaxis(np.asarray(x, np.float32).astype(ml_dtypes.bfloat16).astype(np.float64), axis, -1)
    blocks = v.reshape(v.shape[:-1] + (-1, 32))
    amax = np.abs(blocks).max(-1, keepdims=True)
    byte = np.maximum(np.where(amax > 0, np.frexp(amax)[1] - 1 + 127, 0) - down, 1)
    scale = np.exp2(byte - 127.0)
    codes = (blocks / scale).astype(np.float32).astype(dtype).astype(np.float64)
    return np.moveaxis((codes * scale).reshape(v.shape), -1, axis)


WIDE = False


def mx_kscale(k):
    if not WIDE:
        return np.ones(k)
    levels = np.array([10, -10, 5, -5, 0])
    if k % 512:
        return np.exp2(np.random.permutation(np.resize(levels, k // 32))).repeat(32)
    a = np.empty((k // 512, 16))
    for p in range(k // 512):
        a[p, :8] = np.random.permutation(np.resize(levels, 8))
        for g in range(8):
            far = levels[np.abs(levels - a[p, g]) >= 10]
            a[p, g + 8] = far[np.random.randint(len(far))]
    return np.exp2(a.ravel()).repeat(32)


def f64(x):
    return np.asarray(x).astype(np.float64)


def striped(idx):
    return np.tile(idx.reshape(-1, 16).T, (8, 1)).astype(np.uint16)


def unstriped(offs):
    return offs[:16].T.reshape(-1).astype(np.int64)


def pack_weight(w):
    k, n = w.shape
    w = f64(np.asarray(w, np.float32).astype(ml_dtypes.bfloat16)).reshape(k // 32, 32, n)
    amax = np.abs(w).max(1)
    byte = np.clip(np.where(amax > 0, np.frexp(amax)[1] - 1 + 127 - 7, 1), 1, 254)
    scaled = (w * np.exp2(127.0 - byte)[:, None, :]).reshape(k, n).astype(np.float32)
    words = np.ascontiguousarray(scaled.reshape(k // 512, 128, 4, n).transpose(0, 1, 3, 2)).astype(ml_dtypes.float8_e4m3fn).view(np.uint8)
    return words, np.ascontiguousarray(byte.astype(np.uint8).reshape(k // 512, 16, n))


def unpack_weight(words, scales):
    g, p, n, _ = words.shape
    vals = np.ascontiguousarray(words).view(ml_dtypes.float8_e4m3fn).astype(np.float64) * np.repeat(np.exp2(scales.astype(np.float64) - 127.0), 8, axis=1)[..., None]
    return vals.transpose(0, 1, 3, 2).reshape(g * 512, n)

def planes(y):
    n, m = y.shape
    v = y.astype(np.float32).astype(ml_dtypes.bfloat16).astype(np.float64).reshape(n // 32, 32, m)
    top = np.abs(v).max(1)
    byte = np.clip(np.where(top > 0, np.frexp(top)[1] - 1 + 127 - 7, 1), 1, 254)
    codes = (v * np.exp2(127.0 - byte)[:, None, :]).reshape(n, m).astype(np.float32).astype(ml_dtypes.float8_e4m3fn).view(np.uint8)
    words = codes.reshape(n // 512, 128, 4, m).transpose(0, 1, 3, 2)
    return np.ascontiguousarray(words), np.ascontiguousarray(byte.astype(np.uint8).reshape(n // 512, 16, m))


K, T, S, N, W = 512, 2048, 256, 512, 128


def setup_inputs():
    n = np.random.standard_normal
    s = mx_kscale(K)[:, None]
    packed_xT = pack_weight(n((K, T)) * s)
    perm = np.random.permutation(S)
    return {
        "x_words": packed_xT[0],
        "x_scales": packed_xT[1],
        "w1": (n((K, N)) / np.sqrt(2 * K) / s).astype(np.float32),
        "w2": (n((K, N)) / np.sqrt(2 * K) / s).astype(np.float32),
        "offs": striped(np.random.permutation(T)[:S]),
        "two": striped(np.random.permutation(T)[:S]),
        "n1": striped(perm[:W]),
        "n2": striped(perm[W:]),
    }


def reference(x_words, x_scales, w1, w2, offs, two, n1, n2):
    xq = unpack_weight(x_words, x_scales)[:, unstriped(offs)]
    x_two = unpack_weight(x_words, x_scales)[:, unstriped(two)]
    h = mxq(f64(w1), 0, "e4m3").T @ xq + mxq(f64(w2), 0, "e4m3").T @ x_two
    pa = h[:, unstriped(n1)]
    pb = h[:, unstriped(n2)]
    rb = pa - pb
    ra = 0.75 * (pa + pb)
    ds = np.zeros((N, S))
    ds[:, unstriped(n1)] = ra
    out = ds.copy()
    out[:, unstriped(n2)] = rb
    return (out,) + planes(out)

@@ -1,0 +1,169 @@
+from contextlib import ExitStack
+
+import concourse.mybir as mybir
+
+F32 = mybir.dt.float32
+BF16 = mybir.dt.bfloat16
+I32 = mybir.dt.int32
+U32 = mybir.dt.uint32
+U16 = mybir.dt.uint16
+U8 = mybir.dt.uint8
+FP8X4 = mybir.dt.float8_e4m3fn_x4
+COPY = mybir.ActivationFunctionType.Copy
+ADD = mybir.AluOpType.add
+SUB = mybir.AluOpType.subtract
+
+K, T, S, N, W = 512, 2048, 256, 512, 128
+P = 128
+H = 64
+FLOPS = 2 * 2 * K * N * S
+
+
+def tile_picked_otthaar_none_po_kernel(tc, x_words, x_scales, w1, w2, offs, two, n1, n2, out_0, out_1, out_2):
+    nc = tc.nc
+    with ExitStack() as ctx:
+        keep = ctx.enter_context(tc.tile_pool(name="keep", bufs=1))
+        ring = ctx.enter_context(tc.tile_pool(name="ring", bufs=3))
+        psum = ctx.enter_context(tc.psum_pool(name="psum", bufs=1))
+
+        def tile(shape, dtype, name):
+            return keep.tile(shape, dtype, name=name, align_bytes=64)
+
+        offs_t = keep.tile([P, S // 16], U16, name="offs_t")
+        two_t = keep.tile([P, S // 16], U16, name="two_t")
+        n1_t = keep.tile([P, W // 16], U16, name="n1_t")
+        n2_t = keep.tile([P, W // 16], U16, name="n2_t")
+        xw = tile([P, T], U32, "xw")
+        xs = tile([P, T], U8, "xs")
+
+        nc.vector.memset(xs[:].bitcast(I32), 0)
+        nc.sync.dma_start(offs_t[:], offs)
+        nc.sync.dma_start(two_t[:], two)
+        nc.sync.dma_start(n1_t[:], n1)
+        nc.sync.dma_start(n2_t[:], n2)
+        nc.sync.dma_start(xw[:].bitcast(I32), x_words[0].rearrange("p n t -> p (n t)").bitcast(I32))
+        for q in range(4):
+            nc.scalar.dma_start(xs[32 * q : 32 * q + 4, :].bitcast(I32), x_scales[0, 4 * q : 4 * q + 4, :].bitcast(I32))
+        raw = {}
+
+        def load(i, half):
+            raw[i, half] = ring.tile([P, 4, 256], F32, name="raw")
+            nc.sync.dma_start(raw[i, half][:], (w1, w2)[i].rearrange("(p j) c -> p j c", j=4)[:, :, 256 * half : 256 * half + 256])
+
+        load(0, 0)
+        load(1, 0)
+        load(0, 1)
+
+        gw, gs = [], []
+        for i, lst in enumerate((offs_t, two_t)):
+            gs.append(tile([P, S], U8, f"gs{i}"))
+            nc.vector.tensor_copy(gs[i][:], xs[:].indirect(lst[:]))
+        for i, lst in enumerate((offs_t, two_t)):
+            gw.append(tile([P, S], U32, f"gw{i}"))
+            nc.vector.tensor_copy(gw[i][:], xw[:].indirect(lst[:]))
+
+        early = {}
+        late = [tile([P, 2, P, 4], BF16, f"late{i}") for i in range(2)]
+        codes, scales = {}, {}
+
+        def cast_early(i, half, copy):
+            early[i, half] = tile([P, 2, H, 4], BF16, f"early{i}{half}")
+            src = raw[i, half][:].rearrange("p j (m t) -> p m j t", t=4)[:, :, :, 0:2]
+            copy(early[i, half][:].rearrange("p t m j -> p m j t"), src)
+
+        def quant_early(i, half):
+            codes[i, half] = tile([P, P], U32, f"codes{i}{half}")
+            scales[i, half] = tile([P, P], U8, f"scales{i}{half}")
+            nc.vector.quantize_mx(codes[i, half][:].bitcast(FP8X4), scales[i, half][:], early[i, half][:].rearrange("p t m j -> p (t m j)"))
+
+        def cast_late(i, half, copy):
+            src = raw[i, half][:].rearrange("p j (m t) -> p m j t", t=4)[:, :, :, 2:4]
+            copy(late[i][:, :, H * half : H * half + H, :].rearrange("p t m j -> p m j t"), src)
+
+        def quant_late(i):
+            c = tile([P, 2 * P], U32, f"codesl{i}")
+            s = tile([P, 2 * P], U8, f"scalesl{i}")
+            nc.vector.quantize_mx(c[:].bitcast(FP8X4), s[:], late[i][:].rearrange("p t m j -> p (t m j)"))
+            for t in range(2):
+                codes[i, 2 + t] = c[:, t * P : (t + 1) * P]
+                scales[i, 2 + t] = s[:, t * P : (t + 1) * P]
+
+        h = {}
+
+        def product(u, copy):
+            acc = psum.tile([P, S], F32, name=f"acc{u}")
+            for i in range(2):
+                nc.tensor.matmul_mx(acc[:], lhsT=codes[i, u][:, :].bitcast(FP8X4), lhsT_scale=scales[i, u][:, :],
+                                    rhs=gw[i][:].bitcast(FP8X4), rhs_scale=gs[i][:], start=(i == 0), stop=(i == 1))
+            h[u] = keep.tile([P, S], F32, name=f"h{u}", tag=f"h{u}", align_bytes=64)
+            copy(h[u][:], acc[:])
+
+        pa, pb, ra, rb, y = {}, {}, {}, {}, {}
+
+        def fetch(u):
+            pa[u] = tile([P, W], F32, f"pa{u}")
+            pb[u] = tile([P, W], F32, f"pb{u}")
+            nc.scalar.activation(pa[u][:], h[u][:].indirect(n1_t[:]), COPY)
+            nc.scalar.activation(pb[u][:], h[u][:].indirect(n2_t[:]), COPY)
+            ra[u] = tile([P, W], F32, f"ra{u}")
+            rb[u] = tile([P, W], F32, f"rb{u}")
+            nc.vector.tensor_tensor(ra[u][:], pa[u][:], pb[u][:], ADD)
+            nc.vector.tensor_tensor(rb[u][:], pa[u][:], pb[u][:], SUB)
+
+        def put(u):
+            y[u] = tile([P, S], F32, f"y{u}")
+            nc.scalar.activation(y[u][:].indirect(n1_t[:]), ra[u][:], COPY, scale=0.75)
+            nc.scalar.activation(y[u][:].indirect(n2_t[:]), rb[u][:], COPY)
+
+        rows = out_0.rearrange("(l t) c -> t l c", t=4)
+        pair = tile([P, 2, S], F32, "pair")
+        lo, hi = slice(0, H), slice(H, P)
+
+        cast_early(0, 0, nc.scalar.copy)
+        quant_early(0, 0)
+        cast_late(0, 0, nc.scalar.copy)
+        load(1, 1)
+        cast_early(1, 0, nc.vector.tensor_copy)
+        quant_early(1, 0)
+        cast_late(1, 0, nc.scalar.copy)
+        product(0, nc.scalar.copy)
+        cast_early(0, 1, nc.vector.tensor_copy)
+        quant_early(0, 1)
+        fetch(0)
+        cast_early(1, 1, nc.vector.tensor_copy)
+        quant_early(1, 1)
+        product(1, nc.vector.tensor_copy)
+        put(0)
+        nc.sync.dma_start(pair[lo, 0, :], y[0][lo, :])
+        nc.sync.dma_start(pair[lo, 1, :], y[0][hi, :])
+        cast_late(0, 1, nc.vector.tensor_copy)
+        cast_late(1, 1, nc.vector.tensor_copy)
+        fetch(1)
+        quant_late(0)
+        quant_late(1)
+        product(2, nc.vector.tensor_copy)
+        product(3, nc.vector.tensor_copy)
+        fetch(2)
+        put(1)
+        nc.sync.dma_start(pair[hi, 0, :], y[1][lo, :])
+        nc.sync.dma_start(pair[hi, 1, :], y[1][hi, :])
+        fetch(3)
+        grouped = keep.tile([P, S, 4], BF16, name="grouped", tag="h3", align_bytes=64)
+        nc.sync.dma_start(out_0.rearrange("(l t) c -> l t c", t=4)[:, 0:2, :], pair[:])
+        nc.vector.tensor_copy(grouped[:, :, 0:2], pair[:].rearrange("p t c -> p c t"))
+        put(2)
+        nc.sync.dma_start(rows[2], y[2][:])
+        nc.vector.tensor_copy(grouped[:, :, 2], y[2][:])
+        put(3)
+        nc.sync.dma_start(rows[3], y[3][:])
+        for c in range(2):
+            nc.vector.tensor_copy(grouped[:, c * W : (c + 1) * W, 3], y[3][:, c * W : (c + 1) * W])
+        y_codes = tile([P, S], U32, "y_codes")
+        y_scales = tile([P, S], U8, "y_scales")
+        for c in range(2):
+            cols = slice(c * W, (c + 1) * W)
+            nc.vector.quantize_mx(y_codes[:, cols].bitcast(FP8X4), y_scales[:, cols], grouped[:, cols, :].rearrange("p c t -> p (c t)"))
+        nc.sync.dma_start(out_1[0].rearrange("p c t -> p (c t)").bitcast(I32), y_codes[:].bitcast(I32))
+        for q in range(4):
+            eng = nc.scalar if q % 2 == 0 else nc.sync
+            eng.dma_start(out_2[0, 4 * q : 4 * q + 4, :].bitcast(I32), y_scales[32 * q : 32 * q + 4, :].bitcast(I32))

@@ -11,11 +11,15 @@ U8 = mybir.dt.uint8
 FP8X4 = mybir.dt.float8_e4m3fn_x4
 COPY = mybir.ActivationFunctionType.Copy
 ADD = mybir.AluOpType.add
-SUB = mybir.AluOpType.subtract
+SUBTRACT = mybir.AluOpType.subtract
 
 K, T, S, N, W = 512, 2048, 256, 512, 128
 P = 128
-H = 64
+PACK = 4
+QUADRANTS, QUADRANT, SCALE_ROWS = 4, 32, 4
+ALIGN = 64
+VECTOR_COLUMNS = 80
+HALF = S // 2
 FLOPS = 2 * 2 * K * N * S
 
 
@@ -23,147 +27,124 @@ def tile_picked_otthaar_none_po_kernel(tc, x_words, x_scales, w1, w2, offs, two,
     nc = tc.nc
     with ExitStack() as ctx:
         keep = ctx.enter_context(tc.tile_pool(name="keep", bufs=1))
-        ring = ctx.enter_context(tc.tile_pool(name="ring", bufs=3))
+        shared = ctx.enter_context(tc.tile_pool(name="shared", bufs=1))
         psum = ctx.enter_context(tc.psum_pool(name="psum", bufs=1))
 
         def tile(shape, dtype, name):
-            return keep.tile(shape, dtype, name=name, align_bytes=64)
+            return keep.tile(shape, dtype, name=name, align_bytes=ALIGN)
 
-        offs_t = keep.tile([P, S // 16], U16, name="offs_t")
-        two_t = keep.tile([P, S // 16], U16, name="two_t")
-        n1_t = keep.tile([P, W // 16], U16, name="n1_t")
-        n2_t = keep.tile([P, W // 16], U16, name="n2_t")
-        xw = tile([P, T], U32, "xw")
-        xs = tile([P, T], U8, "xs")
+        def live(q):
+            return slice(QUADRANT * q, QUADRANT * q + SCALE_ROWS)
 
-        nc.vector.memset(xs[:].bitcast(I32), 0)
-        nc.sync.dma_start(offs_t[:], offs)
-        nc.sync.dma_start(two_t[:], two)
-        nc.sync.dma_start(n1_t[:], n1)
-        nc.sync.dma_start(n2_t[:], n2)
-        nc.sync.dma_start(xw[:].bitcast(I32), x_words[0].rearrange("p n t -> p (n t)").bitcast(I32))
-        for q in range(4):
-            nc.scalar.dma_start(xs[32 * q : 32 * q + 4, :].bitcast(I32), x_scales[0, 4 * q : 4 * q + 4, :].bitcast(I32))
-        raw = {}
+        def scale_rows(q):
+            return slice(SCALE_ROWS * q, SCALE_ROWS * (q + 1))
 
-        def load(i, half):
-            raw[i, half] = ring.tile([P, 4, 256], F32, name="raw")
-            nc.sync.dma_start(raw[i, half][:], (w1, w2)[i].rearrange("(p j) c -> p j c", j=4)[:, :, 256 * half : 256 * half + 256])
+        offs_list = keep.tile([P, S // 16], U16, name="offs_list")
+        two_list = keep.tile([P, S // 16], U16, name="two_list")
+        n1_list = keep.tile([P, W // 16], U16, name="n1_list")
+        n2_list = keep.tile([P, W // 16], U16, name="n2_list")
+        pick_lists = (offs_list, two_list)
 
-        load(0, 0)
-        load(1, 0)
-        load(0, 1)
+        scale_window = tile([P, T], U8, "scale_window")
+        scale_landing = tile([P, T], U8, "scale_landing")
+        word_window = tile([P, T], U32, "word_window")
+        raw = [tile([P, PACK, N], F32, f"raw{i}") for i in range(2)]
+        nc.vector.memset(scale_window[:].bitcast(I32), 0)
+        for q in range(QUADRANTS):
+            nc.sync.dma_start(scale_landing[live(q), :].bitcast(I32), x_scales[0, scale_rows(q), :].bitcast(I32))
+        nc.sync.dma_start(raw[0][:], w1.rearrange("(p j) m -> p j m", j=PACK))
+        nc.sync.dma_start(offs_list[:], offs)
+        nc.sync.dma_start(two_list[:], two)
+        nc.sync.dma_start(raw[1][:], w2.rearrange("(p j) m -> p j m", j=PACK))
+        nc.sync.dma_start(word_window[:].bitcast(I32), x_words[0].rearrange("p c j -> p (c j)").bitcast(I32))
+        nc.sync.dma_start(n1_list[:], n1)
+        nc.sync.dma_start(n2_list[:], n2)
 
-        gw, gs = [], []
-        for i, lst in enumerate((offs_t, two_t)):
-            gs.append(tile([P, S], U8, f"gs{i}"))
-            nc.vector.tensor_copy(gs[i][:], xs[:].indirect(lst[:]))
-        for i, lst in enumerate((offs_t, two_t)):
-            gw.append(tile([P, S], U32, f"gw{i}"))
-            nc.vector.tensor_copy(gw[i][:], xw[:].indirect(lst[:]))
+        for q in range(QUADRANTS):
+            nc.vector.tensor_copy(scale_window[live(q), :].bitcast(I32), scale_landing[live(q), :].bitcast(I32))
+        picked_scales = [tile([P, S], U8, f"picked_scales{i}") for i in range(2)]
+        for i in range(2):
+            nc.vector.tensor_copy(picked_scales[i][:], scale_window[:].indirect(pick_lists[i][:]))
 
-        early = {}
-        late = [tile([P, 2, P, 4], BF16, f"late{i}") for i in range(2)]
-        codes, scales = {}, {}
+        dealt_bytes = PACK * P * PACK * 2
+        w_codes, w_scales = [], []
+        for i in range(2):
+            dealt = shared.tile([P, PACK, P, PACK], BF16, name=f"dealt{i}", offset=dealt_bytes * i, align_bytes=ALIGN)
+            source = raw[i][:].rearrange("p j (c t) -> p c j t", t=PACK)
+            target = dealt[:].rearrange("p t c j -> p c j t")
+            nc.vector.tensor_copy(target[:, 0:VECTOR_COLUMNS], source[:, 0:VECTOR_COLUMNS])
+            nc.scalar.copy(target[:, VECTOR_COLUMNS:P], source[:, VECTOR_COLUMNS:P])
+            w_codes.append(tile([P, N], U32, f"w_codes{i}"))
+            w_scales.append(tile([P, N], U8, f"w_scales{i}"))
+            nc.vector.quantize_mx(
+                w_codes[i][:].bitcast(FP8X4), w_scales[i][:], dealt[:].rearrange("p t c j -> p (t c j)")
+            )
 
-        def cast_early(i, half, copy):
-            early[i, half] = tile([P, 2, H, 4], BF16, f"early{i}{half}")
-            src = raw[i, half][:].rearrange("p j (m t) -> p m j t", t=4)[:, :, :, 0:2]
-            copy(early[i, half][:].rearrange("p t m j -> p m j t"), src)
+        picked_words = []
+        for i in range(2):
+            picked_words.append(
+                shared.tile([P, S], U32, name=f"picked_words{i}", offset=dealt_bytes + 4 * S * i, align_bytes=ALIGN)
+            )
+            nc.vector.tensor_copy(picked_words[i][:], word_window[:].indirect(pick_lists[i][:]))
 
-        def quant_early(i, half):
-            codes[i, half] = tile([P, P], U32, f"codes{i}{half}")
-            scales[i, half] = tile([P, P], U8, f"scales{i}{half}")
-            nc.vector.quantize_mx(codes[i, half][:].bitcast(FP8X4), scales[i, half][:], early[i, half][:].rearrange("p t m j -> p (t m j)"))
+        def product(t, cols, order, name):
+            bank = psum.tile([P, cols.stop - cols.start], F32, name=name)
+            operand = slice(t * P, (t + 1) * P)
+            for i in order:
+                nc.tensor.matmul_mx(
+                    bank[:],
+                    lhsT=w_codes[i][:, operand].bitcast(FP8X4),
+                    lhsT_scale=w_scales[i][:, operand],
+                    rhs=picked_words[i][:, cols].bitcast(FP8X4),
+                    rhs_scale=picked_scales[i][:, cols],
+                    start=(i == order[0]),
+                    stop=(i == order[1]),
+                )
+            return bank
 
-        def cast_late(i, half, copy):
-            src = raw[i, half][:].rearrange("p j (m t) -> p m j t", t=4)[:, :, :, 2:4]
-            copy(late[i][:, :, H * half : H * half + H, :].rearrange("p t m j -> p m j t"), src)
+        h = [tile([P, S], F32, f"h{t}") for t in range(PACK)]
+        halves = (slice(0, HALF), slice(HALF, S))
+        for c, copy in enumerate((nc.scalar.copy, nc.vector.tensor_copy)):
+            copy(h[0][:, halves[c]], product(0, halves[c], (0, 1), f"bank0_{c}")[:])
+        for t in range(1, PACK):
+            nc.vector.tensor_copy(h[t][:], product(t, slice(0, S), (1, 0), f"bank{t}")[:])
 
-        def quant_late(i):
-            c = tile([P, 2 * P], U32, f"codesl{i}")
-            s = tile([P, 2 * P], U8, f"scalesl{i}")
-            nc.vector.quantize_mx(c[:].bitcast(FP8X4), s[:], late[i][:].rearrange("p t m j -> p (t m j)"))
-            for t in range(2):
-                codes[i, 2 + t] = c[:, t * P : (t + 1) * P]
-                scales[i, 2 + t] = s[:, t * P : (t + 1) * P]
+        sums = [tile([P, W], F32, f"sum{t}") for t in range(PACK)]
+        differences = [tile([P, W], F32, f"difference{t}") for t in range(PACK)]
+        y = [tile([P, S], F32, f"y{t}") for t in range(PACK)]
+        out_rows = out_0.rearrange("(p t) c -> t p c", t=PACK)
+        grouped = tile([P, S, PACK], BF16, "grouped")
 
-        h = {}
+        def fetch(t):
+            pa = tile([P, W], F32, f"pa{t}")
+            pb = tile([P, W], F32, f"pb{t}")
+            nc.scalar.activation(pa[:], h[t][:].indirect(n1_list[:]), COPY)
+            nc.scalar.activation(pb[:], h[t][:].indirect(n2_list[:]), COPY)
+            nc.vector.tensor_tensor(sums[t][:], pa[:], pb[:], ADD)
+            nc.vector.tensor_tensor(differences[t][:], pa[:], pb[:], SUBTRACT)
 
-        def product(u, copy):
-            acc = psum.tile([P, S], F32, name=f"acc{u}")
-            for i in range(2):
-                nc.tensor.matmul_mx(acc[:], lhsT=codes[i, u][:, :].bitcast(FP8X4), lhsT_scale=scales[i, u][:, :],
-                                    rhs=gw[i][:].bitcast(FP8X4), rhs_scale=gs[i][:], start=(i == 0), stop=(i == 1))
-            h[u] = keep.tile([P, S], F32, name=f"h{u}", tag=f"h{u}", align_bytes=64)
-            copy(h[u][:], acc[:])
+        def put(t):
+            nc.scalar.activation(y[t][:].indirect(n1_list[:]), sums[t][:], COPY, scale=0.75)
+            nc.scalar.activation(y[t][:].indirect(n2_list[:]), differences[t][:], COPY)
+            nc.sync.dma_start(out_rows[t], y[t][:])
 
-        pa, pb, ra, rb, y = {}, {}, {}, {}, {}
-
-        def fetch(u):
-            pa[u] = tile([P, W], F32, f"pa{u}")
-            pb[u] = tile([P, W], F32, f"pb{u}")
-            nc.scalar.activation(pa[u][:], h[u][:].indirect(n1_t[:]), COPY)
-            nc.scalar.activation(pb[u][:], h[u][:].indirect(n2_t[:]), COPY)
-            ra[u] = tile([P, W], F32, f"ra{u}")
-            rb[u] = tile([P, W], F32, f"rb{u}")
-            nc.vector.tensor_tensor(ra[u][:], pa[u][:], pb[u][:], ADD)
-            nc.vector.tensor_tensor(rb[u][:], pa[u][:], pb[u][:], SUB)
-
-        def put(u):
-            y[u] = tile([P, S], F32, f"y{u}")
-            nc.scalar.activation(y[u][:].indirect(n1_t[:]), ra[u][:], COPY, scale=0.75)
-            nc.scalar.activation(y[u][:].indirect(n2_t[:]), rb[u][:], COPY)
-
-        rows = out_0.rearrange("(l t) c -> t l c", t=4)
-        pair = tile([P, 2, S], F32, "pair")
-        lo, hi = slice(0, H), slice(H, P)
-
-        cast_early(0, 0, nc.scalar.copy)
-        quant_early(0, 0)
-        cast_late(0, 0, nc.scalar.copy)
-        load(1, 1)
-        cast_early(1, 0, nc.vector.tensor_copy)
-        quant_early(1, 0)
-        cast_late(1, 0, nc.scalar.copy)
-        product(0, nc.scalar.copy)
-        cast_early(0, 1, nc.vector.tensor_copy)
-        quant_early(0, 1)
+        last = PACK - 1
         fetch(0)
-        cast_early(1, 1, nc.vector.tensor_copy)
-        quant_early(1, 1)
-        product(1, nc.vector.tensor_copy)
-        put(0)
-        nc.sync.dma_start(pair[lo, 0, :], y[0][lo, :])
-        nc.sync.dma_start(pair[lo, 1, :], y[0][hi, :])
-        cast_late(0, 1, nc.vector.tensor_copy)
-        cast_late(1, 1, nc.vector.tensor_copy)
-        fetch(1)
-        quant_late(0)
-        quant_late(1)
-        product(2, nc.vector.tensor_copy)
-        product(3, nc.vector.tensor_copy)
-        fetch(2)
-        put(1)
-        nc.sync.dma_start(pair[hi, 0, :], y[1][lo, :])
-        nc.sync.dma_start(pair[hi, 1, :], y[1][hi, :])
-        fetch(3)
-        grouped = keep.tile([P, S, 4], BF16, name="grouped", tag="h3", align_bytes=64)
-        nc.sync.dma_start(out_0.rearrange("(l t) c -> l t c", t=4)[:, 0:2, :], pair[:])
-        nc.vector.tensor_copy(grouped[:, :, 0:2], pair[:].rearrange("p t c -> p c t"))
-        put(2)
-        nc.sync.dma_start(rows[2], y[2][:])
-        nc.vector.tensor_copy(grouped[:, :, 2], y[2][:])
-        put(3)
-        nc.sync.dma_start(rows[3], y[3][:])
-        for c in range(2):
-            nc.vector.tensor_copy(grouped[:, c * W : (c + 1) * W, 3], y[3][:, c * W : (c + 1) * W])
+        for t in range(last):
+            fetch(t + 1)
+            put(t)
+            nc.vector.tensor_copy(grouped[:, :, t], y[t][:])
+        put(last)
+
         y_codes = tile([P, S], U32, "y_codes")
         y_scales = tile([P, S], U8, "y_scales")
-        for c in range(2):
-            cols = slice(c * W, (c + 1) * W)
-            nc.vector.quantize_mx(y_codes[:, cols].bitcast(FP8X4), y_scales[:, cols], grouped[:, cols, :].rearrange("p c t -> p (c t)"))
+        for cols in halves:
+            nc.vector.tensor_copy(grouped[:, cols, last], y[last][:, cols])
+        for cols in halves:
+            nc.vector.quantize_mx(
+                y_codes[:, cols].bitcast(FP8X4), y_scales[:, cols], grouped[:, cols, :].rearrange("p c t -> p (c t)")
+            )
         nc.sync.dma_start(out_1[0].rearrange("p c t -> p (c t)").bitcast(I32), y_codes[:].bitcast(I32))
-        for q in range(4):
-            eng = nc.scalar if q % 2 == 0 else nc.sync
-            eng.dma_start(out_2[0, 4 * q : 4 * q + 4, :].bitcast(I32), y_scales[32 * q : 32 * q + 4, :].bitcast(I32))
+        for q in range(QUADRANTS):
+            queue = nc.scalar if q % 2 == 0 else nc.sync
+            queue.dma_start(out_2[0, scale_rows(q), :].bitcast(I32), y_scales[live(q), :].bitcast(I32))

from contextlib import ExitStack

import concourse.mybir as mybir

F32 = mybir.dt.float32
BF16 = mybir.dt.bfloat16
I32 = mybir.dt.int32
U32 = mybir.dt.uint32
U16 = mybir.dt.uint16
U8 = mybir.dt.uint8
FP8X4 = mybir.dt.float8_e4m3fn_x4
COPY = mybir.ActivationFunctionType.Copy
ADD = mybir.AluOpType.add
SUBTRACT = mybir.AluOpType.subtract

K, T, S, N, W = 512, 2048, 256, 512, 128
P = 128
PACK = 4
QUADRANTS, QUADRANT, SCALE_ROWS = 4, 32, 4
ALIGN = 64
VECTOR_COLUMNS = 80
HALF = S // 2
FLOPS = 2 * 2 * K * N * S


def tile_picked_otthaar_none_po_kernel(tc, x_words, x_scales, w1, w2, offs, two, n1, n2, out_0, out_1, out_2):
    nc = tc.nc
    with ExitStack() as ctx:
        keep = ctx.enter_context(tc.tile_pool(name="keep", bufs=1))
        shared = ctx.enter_context(tc.tile_pool(name="shared", bufs=1))
        psum = ctx.enter_context(tc.psum_pool(name="psum", bufs=1))

        def tile(shape, dtype, name):
            return keep.tile(shape, dtype, name=name, align_bytes=ALIGN)

        def live(q):
            return slice(QUADRANT * q, QUADRANT * q + SCALE_ROWS)

        def scale_rows(q):
            return slice(SCALE_ROWS * q, SCALE_ROWS * (q + 1))

        offs_list = keep.tile([P, S // 16], U16, name="offs_list")
        two_list = keep.tile([P, S // 16], U16, name="two_list")
        n1_list = keep.tile([P, W // 16], U16, name="n1_list")
        n2_list = keep.tile([P, W // 16], U16, name="n2_list")
        pick_lists = (offs_list, two_list)

        scale_window = tile([P, T], U8, "scale_window")
        scale_landing = tile([P, T], U8, "scale_landing")
        word_window = tile([P, T], U32, "word_window")
        raw = [tile([P, PACK, N], F32, f"raw{i}") for i in range(2)]
        nc.vector.memset(scale_window[:].bitcast(I32), 0)
        for q in range(QUADRANTS):
            nc.sync.dma_start(scale_landing[live(q), :].bitcast(I32), x_scales[0, scale_rows(q), :].bitcast(I32))
        nc.sync.dma_start(raw[0][:], w1.rearrange("(p j) m -> p j m", j=PACK))
        nc.sync.dma_start(offs_list[:], offs)
        nc.sync.dma_start(two_list[:], two)
        nc.sync.dma_start(raw[1][:], w2.rearrange("(p j) m -> p j m", j=PACK))
        nc.sync.dma_start(word_window[:].bitcast(I32), x_words[0].rearrange("p c j -> p (c j)").bitcast(I32))
        nc.sync.dma_start(n1_list[:], n1)
        nc.sync.dma_start(n2_list[:], n2)

        for q in range(QUADRANTS):
            nc.vector.tensor_copy(scale_window[live(q), :].bitcast(I32), scale_landing[live(q), :].bitcast(I32))
        picked_scales = [tile([P, S], U8, f"picked_scales{i}") for i in range(2)]
        for i in range(2):
            nc.vector.tensor_copy(picked_scales[i][:], scale_window[:].indirect(pick_lists[i][:]))

        dealt_bytes = PACK * P * PACK * 2
        w_codes, w_scales = [], []
        for i in range(2):
            dealt = shared.tile([P, PACK, P, PACK], BF16, name=f"dealt{i}", offset=dealt_bytes * i, align_bytes=ALIGN)
            source = raw[i][:].rearrange("p j (c t) -> p c j t", t=PACK)
            target = dealt[:].rearrange("p t c j -> p c j t")
            nc.vector.tensor_copy(target[:, 0:VECTOR_COLUMNS], source[:, 0:VECTOR_COLUMNS])
            nc.scalar.copy(target[:, VECTOR_COLUMNS:P], source[:, VECTOR_COLUMNS:P])
            w_codes.append(tile([P, N], U32, f"w_codes{i}"))
            w_scales.append(tile([P, N], U8, f"w_scales{i}"))
            nc.vector.quantize_mx(
                w_codes[i][:].bitcast(FP8X4), w_scales[i][:], dealt[:].rearrange("p t c j -> p (t c j)")
            )

        picked_words = []
        for i in range(2):
            picked_words.append(
                shared.tile([P, S], U32, name=f"picked_words{i}", offset=dealt_bytes + 4 * S * i, align_bytes=ALIGN)
            )
            nc.vector.tensor_copy(picked_words[i][:], word_window[:].indirect(pick_lists[i][:]))

        def product(t, cols, order, name):
            bank = psum.tile([P, cols.stop - cols.start], F32, name=name)
            operand = slice(t * P, (t + 1) * P)
            for i in order:
                nc.tensor.matmul_mx(
                    bank[:],
                    lhsT=w_codes[i][:, operand].bitcast(FP8X4),
                    lhsT_scale=w_scales[i][:, operand],
                    rhs=picked_words[i][:, cols].bitcast(FP8X4),
                    rhs_scale=picked_scales[i][:, cols],
                    start=(i == order[0]),
                    stop=(i == order[1]),
                )
            return bank

        h = [tile([P, S], F32, f"h{t}") for t in range(PACK)]
        halves = (slice(0, HALF), slice(HALF, S))
        for c, copy in enumerate((nc.scalar.copy, nc.vector.tensor_copy)):
            copy(h[0][:, halves[c]], product(0, halves[c], (0, 1), f"bank0_{c}")[:])
        for t in range(1, PACK):
            nc.vector.tensor_copy(h[t][:], product(t, slice(0, S), (1, 0), f"bank{t}")[:])

        sums = [tile([P, W], F32, f"sum{t}") for t in range(PACK)]
        differences = [tile([P, W], F32, f"difference{t}") for t in range(PACK)]
        y = [tile([P, S], F32, f"y{t}") for t in range(PACK)]
        out_rows = out_0.rearrange("(p t) c -> t p c", t=PACK)
        grouped = tile([P, S, PACK], BF16, "grouped")

        def fetch(t):
            pa = tile([P, W], F32, f"pa{t}")
            pb = tile([P, W], F32, f"pb{t}")
            nc.scalar.activation(pa[:], h[t][:].indirect(n1_list[:]), COPY)
            nc.scalar.activation(pb[:], h[t][:].indirect(n2_list[:]), COPY)
            nc.vector.tensor_tensor(sums[t][:], pa[:], pb[:], ADD)
            nc.vector.tensor_tensor(differences[t][:], pa[:], pb[:], SUBTRACT)

        def put(t):
            nc.scalar.activation(y[t][:].indirect(n1_list[:]), sums[t][:], COPY, scale=0.75)
            nc.scalar.activation(y[t][:].indirect(n2_list[:]), differences[t][:], COPY)
            nc.sync.dma_start(out_rows[t], y[t][:])

        last = PACK - 1
        fetch(0)
        for t in range(last):
            fetch(t + 1)
            put(t)
            nc.vector.tensor_copy(grouped[:, :, t], y[t][:])
        put(last)

        y_codes = tile([P, S], U32, "y_codes")
        y_scales = tile([P, S], U8, "y_scales")
        for cols in halves:
            nc.vector.tensor_copy(grouped[:, cols, last], y[last][:, cols])
        for cols in halves:
            nc.vector.quantize_mx(
                y_codes[:, cols].bitcast(FP8X4), y_scales[:, cols], grouped[:, cols, :].rearrange("p c t -> p (c t)")
            )
        nc.sync.dma_start(out_1[0].rearrange("p c t -> p (c t)").bitcast(I32), y_codes[:].bitcast(I32))
        for q in range(QUADRANTS):
            queue = nc.scalar if q % 2 == 0 else nc.sync
            queue.dma_start(out_2[0, scale_rows(q), :].bitcast(I32), y_scales[live(q), :].bitcast(I32))
